import numpy as np
import ml_dtypes


def mxq(x, axis, fmt="e4m3"):
    dtype, down = {"e4m3": (ml_dtypes.float8_e4m3fn, 7), "e5m2": (ml_dtypes.float8_e5m2, 14)}[fmt]
    v = np.moveaxis(np.asarray(x, np.float32).astype(ml_dtypes.bfloat16).astype(np.float64), axis, -1)
    blocks = v.reshape(v.shape[:-1] + (-1, 32))
    amax = np.abs(blocks).max(-1, keepdims=True)
    byte = np.maximum(np.where(amax > 0, np.frexp(amax)[1] - 1 + 127, 0) - down, 1)
    scale = np.exp2(byte - 127.0)
    codes = (blocks / scale).astype(np.float32).astype(dtype).astype(np.float64)
    return np.moveaxis((codes * scale).reshape(v.shape), -1, axis)


WIDE = False


def mx_kscale(k):
    if not WIDE:
        return np.ones(k)
    levels = np.array([10, -10, 5, -5, 0])
    if k % 512:
        return np.exp2(np.random.permutation(np.resize(levels, k // 32))).repeat(32)
    a = np.empty((k // 512, 16))
    for p in range(k // 512):
        a[p, :8] = np.random.permutation(np.resize(levels, 8))
        for g in range(8):
            far = levels[np.abs(levels - a[p, g]) >= 10]
            a[p, g + 8] = far[np.random.randint(len(far))]
    return np.exp2(a.ravel()).repeat(32)


def f64(x):
    return np.asarray(x).astype(np.float64)


def striped(idx):
    return np.tile(np.asarray(idx).reshape(-1, 16).T, (8, 1)).astype(np.uint16)


def unstriped(offs):
    return offs[:16].T.reshape(-1).astype(np.int64)


E2M1 = np.array([0.0, 0.5, 1.0, 1.5, 2.0, 3.0, 4.0, 6.0, -0.0, -0.5, -1.0, -1.5, -2.0, -3.0, -4.0, -6.0])


def pack_weight(w, fmt):
    k, n = w.shape
    w = f64(np.asarray(w, np.float32).astype(ml_dtypes.bfloat16)).reshape(k // 32, 32, n)
    amax = np.abs(w).max(1)
    if fmt == "e4m3":
        byte = np.frexp(amax)[1] - 1 + 127 - 7
    else:
        mant, ex = np.frexp(amax / 6.0)
        byte = np.where(mant > 0.5, ex, ex - 1) + 127
    byte = np.clip(np.where(amax > 0, byte, 1), 1, 254)
    scaled = (w * np.exp2(127.0 - byte)[:, None, :]).reshape(k, n).astype(np.float32)
    by_word = np.ascontiguousarray(scaled.reshape(k // 512, 128, 4, n).transpose(0, 1, 3, 2))
    if fmt == "e4m3":
        words = by_word.astype(ml_dtypes.float8_e4m3fn).view(np.uint8)
    else:
        c = by_word.astype(ml_dtypes.float4_e2m1fn).view(np.uint8) & 0xF
        words = (c[..., 0::2] | (c[..., 1::2] << 4)).reshape(k // 512, 128, 2 * n)
    return np.ascontiguousarray(words), np.ascontiguousarray(byte.astype(np.uint8).reshape(k // 512, 16, n))


def unpack_weight(words, scales, fmt):
    g, _, n = scales.shape
    words = np.ascontiguousarray(words).reshape(g, 128, n, -1)
    if fmt == "e4m3":
        vals = words.view(ml_dtypes.float8_e4m3fn).astype(np.float64)
    else:
        nib = np.empty((g, 128, n, 4), np.uint8)
        nib[..., 0::2] = words & 0xF
        nib[..., 1::2] = words >> 4
        vals = E2M1[nib]
    vals = vals * np.repeat(np.exp2(scales.astype(np.float64) - 127.0), 8, axis=1)[..., None]
    return vals.transpose(0, 1, 3, 2).reshape(g * 512, n)


B, N, T, D, NQ = 1, 512, 2048, 512, 512
DV = 512


def sgn(shape):
    return np.random.uniform(0.5, 2.0, shape) * np.where(np.random.standard_normal(shape) < 0, -1.0, 1.0)


def setup_inputs():
    n = np.random.standard_normal
    idx = np.random.permutation(T)[:B * N]
    s = mx_kscale(D)[:, None]
    u = mx_kscale(N)
    ut = np.ones(T)
    ut[idx] = u
    kp = pack_weight(n((D, T)) / s, "e4m3")
    return {
        "qT": (n((B, D, NQ)) * s * (1.00 / np.sqrt(D))).astype(np.float32),
        "k_words": kp[0],
        "k_scales": kp[1],
        "vT": (n((DV, T)) / ut).astype(np.float32),
        "nb": np.tile(0.5 * n(2048), (128, 1)).astype(np.float32),
        "us": (sgn((B, N, 1)) * u[:, None]).astype(np.float32),
        "offs": striped(idx),
    }


def reference(qT, k_words, k_scales, vT, nb, us, offs):
    idx = unstriped(offs)
    pick = lambda x, which: x[:, which].reshape(x.shape[0], B, -1).transpose(1, 0, 2)
    k = unpack_weight(k_words, k_scales, "e4m3")
    kg = pick(k, idx)
    qq = mxq(f64(qT), 1, "e4m3")
    a = kg.transpose(0, 2, 1) @ qq
    y = np.maximum(a + pick(f64(nb), idx)[:, :1, :].transpose(0, 2, 1), 0.0) * f64(us)
    wq = mxq(y, 1, "e4m3")
    o = wq.transpose(0, 2, 1) @ mxq(pick(f64(vT), idx).transpose(0, 2, 1), 1, "e4m3")
    return o

@@ -1,0 +1,190 @@
+from contextlib import ExitStack
+
+import concourse.mybir as mybir
+from concourse.masks import make_identity
+
+T, D, NQ, N, DV = 2048, 512, 512, 512, 512
+FLOPS = 2 * N * D * NQ + 2 * NQ * N * DV
+
+F32 = mybir.dt.float32
+BF16 = mybir.dt.bfloat16
+I32 = mybir.dt.int32
+U32 = mybir.dt.uint32
+U16 = mybir.dt.uint16
+U8 = mybir.dt.uint8
+FP8X4 = mybir.dt.float8_e4m3fn_x4
+ACT = mybir.ActivationFunctionType
+MULT = mybir.AluOpType.mult
+
+P = 128
+PACK = 4
+HALVES = 2
+QH = NQ // HALVES
+E_BLOCKS = DV // P
+Q_BLOCKS = NQ // P
+NB_ROW = 16
+
+
+def tile_attend_mlpb_relu_topk_kernel(tc, qT, k_words, k_scales, vT, nb, us, offs, out):
+    nc = tc.nc
+    with ExitStack() as ctx:
+        sb = ctx.enter_context(tc.tile_pool(name="sb", bufs=1))
+        ps = ctx.enter_context(tc.psum_pool(name="ps", bufs=1))
+
+        offsets = sb.tile([P, N // 16], U16, name="offsets")
+        nc.sync.dma_start(offsets[:], offs)
+        kw_pool = sb.tile([P, T], I32, name="kw_pool", tag="stage1")
+        nc.sync.dma_start(kw_pool[:], k_words[0].rearrange("p n t -> p (n t)").bitcast(I32))
+        q_raw = sb.tile([P, PACK, NQ], F32, name="q_raw")
+        nc.sync.dma_start(q_raw[:], qT[0].rearrange("(p t) q -> p t q", t=PACK))
+
+        ks_pool = sb.tile([P, T], U8, name="ks_pool", tag="stage3")
+        nc.vector.memset(ks_pool[:].bitcast(I32), 0)
+        nb_pool = sb.tile([P, T], F32, name="nb_pool")
+        nc.vector.memset(nb_pool[:], 0.0)
+        us_col = sb.tile([P, PACK], F32, name="us_col", tag="stage0")
+        nc.scalar.dma_start(us_col[:], us[0].rearrange("(p t) o -> p (t o)", t=PACK))
+        for quad in range(4):
+            nc.scalar.dma_start(
+                ks_pool[32 * quad : 32 * quad + 4, :].bitcast(I32),
+                k_scales[0][4 * quad : 4 * quad + 4, :].bitcast(I32),
+            )
+        nc.scalar.dma_start(nb_pool[NB_ROW : NB_ROW + 1, :], nb[NB_ROW : NB_ROW + 1, :])
+
+        ident = sb.tile([P, P], F32, name="ident")
+        make_identity(nc, ident[:])
+
+        us_abs = sb.tile([P, PACK], F32, name="us_abs")
+        nc.scalar.activation(us_abs[:], us_col[:], ACT.Abs)
+        us_sign = sb.tile([P, PACK], BF16, name="us_sign")
+        nc.scalar.activation(us_sign[:], us_col[:], ACT.Sign)
+
+        v_pool = []
+
+        def load_values(j):
+            v_tile = sb.tile([P, T], F32, name=f"v_pool{j}", tag=f"stage{j}")
+            nc.sync.dma_start(v_tile[:], vT[j * P : (j + 1) * P, :])
+            v_pool.append(v_tile)
+
+        kw_listed = sb.tile([P, N], U32, name="kw_listed", tag="stage2")
+        nc.vector.tensor_copy(kw_listed[:], kw_pool[:].bitcast(U32).indirect(offsets[:]))
+        kw_dealt = sb.tile([P, N], U32, name="kw_dealt", align_bytes=64)
+        nc.vector.tensor_copy(
+            kw_dealt[:].bitcast(I32).rearrange("p (t s) -> p s t", t=PACK),
+            kw_listed[:].bitcast(I32).rearrange("p (s t) -> p s t", t=PACK),
+        )
+
+        load_values(0)
+        load_values(1)
+        load_values(2)
+
+        ks_listed = sb.tile([P, N], U8, name="ks_listed")
+        nc.vector.tensor_copy(ks_listed[:], ks_pool[:].indirect(offsets[:]))
+        load_values(3)
+        ks_dealt = sb.tile([P, N], U8, name="ks_dealt", align_bytes=64)
+        nc.vector.tensor_copy(
+            ks_dealt[:].rearrange("p (t s) -> p s t", t=PACK),
+            ks_listed[:].rearrange("p (s t) -> p s t", t=PACK),
+        )
+        nb_listed = sb.tile([P, N], F32, name="nb_listed")
+        nc.vector.tensor_copy(nb_listed[:], nb_pool[:].indirect(offsets[:]))
+
+        nb_turned = ps.tile([P, PACK, P], F32, name="nb_turned")
+        for t in range(PACK):
+            nc.tensor.transpose(nb_turned[:, t, :], nb_listed[:, t::PACK], ident[:])
+        bias = sb.tile([P, PACK], F32, name="bias")
+        nc.vector.tensor_tensor(bias[:], nb_turned[:, :, NB_ROW], us_abs[:], MULT)
+
+        q_codes, q_scales = [], []
+        for h in range(HALVES):
+            q_woven = sb.tile([P, QH, PACK], BF16, name=f"q_woven{h}", align_bytes=64)
+            nc.scalar.copy(
+                q_woven[:].rearrange("p (c i) t -> p c t i", i=4),
+                q_raw[:, :, h * QH : (h + 1) * QH].rearrange("p t (c i) -> p c t i", i=4),
+            )
+            codes = sb.tile([P, QH], U32, name=f"q_codes{h}", align_bytes=64)
+            scales = sb.tile([P, QH], U8, name=f"q_scales{h}", align_bytes=64)
+            nc.vector.quantize_mx(codes[:].bitcast(FP8X4), scales[:], q_woven[:].rearrange("p q t -> p (q t)"))
+            q_codes.append(codes)
+            q_scales.append(scales)
+
+        y_codes, y_scales = [], []
+        v_codes, v_scales = [], []
+
+        def first_layer(h):
+            pairs = sb.tile([P, 2, QH, 2], BF16, name=f"y_pairs{h}")
+            for t in range(PACK):
+                a = ps.tile([P, QH], F32, name=f"bank{t}")
+                nc.tensor.matmul_mx(
+                    a[:],
+                    lhsT=kw_dealt[:, t * P : (t + 1) * P].bitcast(FP8X4),
+                    lhsT_scale=ks_dealt[:, t * P : (t + 1) * P],
+                    rhs=q_codes[h][:].bitcast(FP8X4),
+                    rhs_scale=q_scales[h][:],
+                    start=True,
+                    stop=True,
+                )
+                nc.scalar.activation(
+                    pairs[:, t // 2, :, t % 2], a[:], ACT.Relu, bias=bias[:, t : t + 1], scale=us_abs[:, t : t + 1]
+                )
+            woven = sb.tile([P, QH, 2, 2], BF16, name=f"y_woven{h}", align_bytes=64)
+            nc.vector.tensor_tensor(
+                woven[:],
+                pairs[:].rearrange("p u q e -> p q u e"),
+                us_sign[:].rearrange("p (u e) -> p u e", e=2).unsqueeze(1).to_broadcast([P, QH, 2, 2]),
+                MULT,
+            )
+            codes = sb.tile([P, QH], U32, name=f"y_codes{h}", align_bytes=64)
+            scales = sb.tile([P, QH], U8, name=f"y_scales{h}", align_bytes=64)
+            nc.vector.quantize_mx(codes[:].bitcast(FP8X4), scales[:], woven[:].rearrange("p q u e -> p (q u e)"))
+            y_codes.append(codes)
+            y_scales.append(scales)
+
+        def values(j):
+            listed = sb.tile([P, N], BF16, name=f"v_listed{j}")
+            nc.vector.tensor_copy(listed[:], v_pool[j][:].indirect(offsets[:]))
+            words = listed[:].bitcast(F32)
+            turned = ps.tile([P, 2, P], F32, name=f"v_turned{j % 2}")
+            for u in range(2):
+                nc.tensor.transpose(turned[:, u, :], words[:, u::2], ident[:])
+            woven = sb.tile([P, P * PACK], BF16, name=f"v_woven{j}", align_bytes=64)
+            nc.scalar.copy(
+                woven[:].bitcast(F32).rearrange("p (e u) -> p e u", u=2),
+                turned[:].rearrange("p u e -> p e u"),
+            )
+            codes = sb.tile([P, P], U32, name=f"v_codes{j}", align_bytes=64)
+            scales = sb.tile([P, P], U8, name=f"v_scales{j}", align_bytes=64)
+            nc.vector.quantize_mx(codes[:].bitcast(FP8X4), scales[:], woven[:])
+            v_codes.append(codes)
+            v_scales.append(scales)
+
+        out_rows = out[0].rearrange("(b p) e -> p b e", p=P)
+
+        def second_layer(j, blocks, bank, copy, queue):
+            o = ps.tile([P, len(blocks), P], F32, name=f"bank{bank}")
+            for n, b in enumerate(blocks):
+                h, c = divmod(b * P, QH)
+                nc.tensor.matmul_mx(
+                    o[:, n, :],
+                    lhsT=y_codes[h][:, c : c + P].bitcast(FP8X4),
+                    lhsT_scale=y_scales[h][:, c : c + P],
+                    rhs=v_codes[j][:].bitcast(FP8X4),
+                    rhs_scale=v_scales[j][:],
+                    start=True,
+                    stop=True,
+                )
+            staged = sb.tile([P, len(blocks), P], F32, name=f"staged{j}_{blocks[0]}")
+            copy(staged[:], o[:])
+            queue.dma_start(out_rows[:, blocks[0] : blocks[-1] + 1, j * P : (j + 1) * P], staged[:])
+
+        first_layer(0)
+        values(0)
+        first_layer(1)
+        values(1)
+        second_layer(0, [0, 1, 2, 3], 0, nc.scalar.copy, nc.sync)
+        second_layer(1, [0, 1, 2, 3], 1, nc.scalar.copy, nc.sync)
+        values(2)
+        second_layer(2, [0, 1, 2, 3], 2, nc.scalar.copy, nc.sync)
+        values(3)
+        second_layer(3, [0, 1], 3, nc.scalar.copy, nc.scalar)
+        second_layer(3, [2, 3], 0, nc.vector.tensor_copy, nc.sync)

@@ -1,7 +1,6 @@
 from contextlib import ExitStack
 
 import concourse.mybir as mybir
-from concourse.masks import make_identity
 
 T, D, NQ, N, DV = 2048, 512, 512, 512, 512
 FLOPS = 2 * N * D * NQ + 2 * NQ * N * DV
@@ -14,7 +13,7 @@ U16 = mybir.dt.uint16
 U8 = mybir.dt.uint8
 FP8X4 = mybir.dt.float8_e4m3fn_x4
 ACT = mybir.ActivationFunctionType
-MULT = mybir.AluOpType.mult
+ALU = mybir.AluOpType
 
 P = 128
 PACK = 4
@@ -29,162 +28,192 @@ def tile_attend_mlpb_relu_topk_kernel(tc, qT, k_words, k_scales, vT, nb, us, off
     nc = tc.nc
     with ExitStack() as ctx:
         sb = ctx.enter_context(tc.tile_pool(name="sb", bufs=1))
+        area = ctx.enter_context(tc.tile_pool(name="area", bufs=1))
         ps = ctx.enter_context(tc.psum_pool(name="ps", bufs=1))
+
+        def staged_tile(shape, dtype, name, buffer):
+            if isinstance(buffer, int):
+                return area.tile(shape, dtype, name=name, offset=buffer * T * 4, align_bytes=64)
+            return sb.tile(shape, dtype, name=name, tag=buffer, align_bytes=64)
 
         offsets = sb.tile([P, N // 16], U16, name="offsets")
         nc.sync.dma_start(offsets[:], offs)
-        kw_pool = sb.tile([P, T], I32, name="kw_pool", tag="stage1")
-        nc.sync.dma_start(kw_pool[:], k_words[0].rearrange("p n t -> p (n t)").bitcast(I32))
-        q_raw = sb.tile([P, PACK, NQ], F32, name="q_raw")
+        q_raw = staged_tile([P, PACK, NQ], F32, "q_raw", "d")
         nc.sync.dma_start(q_raw[:], qT[0].rearrange("(p t) q -> p t q", t=PACK))
 
-        ks_pool = sb.tile([P, T], U8, name="ks_pool", tag="stage3")
+        ks_pool = staged_tile([P, T], U8, "ks_pool", "b")
         nc.vector.memset(ks_pool[:].bitcast(I32), 0)
-        nb_pool = sb.tile([P, T], F32, name="nb_pool")
+        nb_pool = staged_tile([P, T], F32, "nb_pool", "c")
         nc.vector.memset(nb_pool[:], 0.0)
-        us_col = sb.tile([P, PACK], F32, name="us_col", tag="stage0")
+        us_col = staged_tile([P, PACK], F32, "us_col", "a")
         nc.scalar.dma_start(us_col[:], us[0].rearrange("(p t) o -> p (t o)", t=PACK))
         for quad in range(4):
             nc.scalar.dma_start(
                 ks_pool[32 * quad : 32 * quad + 4, :].bitcast(I32),
                 k_scales[0][4 * quad : 4 * quad + 4, :].bitcast(I32),
             )
-        nc.scalar.dma_start(nb_pool[NB_ROW : NB_ROW + 1, :], nb[NB_ROW : NB_ROW + 1, :])
+        nc.sync.dma_start(nb_pool[NB_ROW : NB_ROW + 1, :], nb[NB_ROW : NB_ROW + 1, :])
 
+        zeros = staged_tile([P, 5 * T], F32, "zeros", 0)
+        nc.vector.memset(zeros[:, :P], 0.0)
         ident = sb.tile([P, P], F32, name="ident")
-        make_identity(nc, ident[:])
+        nc.gpsimd.affine_select(
+            out=ident[:],
+            in_=zeros[:, :P],
+            compare_op=ALU.not_equal,
+            fill=1.0,
+            base=0,
+            pattern=[[-1, P]],
+            channel_multiplier=1,
+        )
+        kw_pool = staged_tile([P, T], I32, "kw_pool", 0)
+        nc.sync.dma_start(kw_pool[:], k_words[0].rearrange("p n t -> p (n t)").bitcast(I32))
 
-        us_abs = sb.tile([P, PACK], F32, name="us_abs")
-        nc.scalar.activation(us_abs[:], us_col[:], ACT.Abs)
+        us_step = sb.tile([P, PACK], F32, name="us_step")
+        nc.vector.tensor_scalar(us_step[:], us_col[:], 0.0, 2.0, ALU.is_ge, ALU.mult)
         us_sign = sb.tile([P, PACK], BF16, name="us_sign")
-        nc.scalar.activation(us_sign[:], us_col[:], ACT.Sign)
+        nc.vector.tensor_scalar(us_sign[:], us_step[:], 1.0, -1.0, ALU.mult, ALU.add)
+        us_abs = sb.tile([P, PACK], F32, name="us_abs")
+        nc.vector.tensor_tensor(us_abs[:], us_col[:], us_sign[:], ALU.mult)
 
         v_pool = []
 
-        def load_values(j):
-            v_tile = sb.tile([P, T], F32, name=f"v_pool{j}", tag=f"stage{j}")
+        def load_values(buffer):
+            j = len(v_pool)
+            v_tile = staged_tile([P, T], F32, f"v_pool{j}", buffer)
             nc.sync.dma_start(v_tile[:], vT[j * P : (j + 1) * P, :])
             v_pool.append(v_tile)
 
-        kw_listed = sb.tile([P, N], U32, name="kw_listed", tag="stage2")
-        nc.vector.tensor_copy(kw_listed[:], kw_pool[:].bitcast(U32).indirect(offsets[:]))
-        kw_dealt = sb.tile([P, N], U32, name="kw_dealt", align_bytes=64)
-        nc.vector.tensor_copy(
-            kw_dealt[:].bitcast(I32).rearrange("p (t s) -> p s t", t=PACK),
-            kw_listed[:].bitcast(I32).rearrange("p (s t) -> p s t", t=PACK),
-        )
-
-        load_values(0)
-        load_values(1)
-        load_values(2)
+        for j in range(E_BLOCKS):
+            load_values(1 + j)
 
         ks_listed = sb.tile([P, N], U8, name="ks_listed")
         nc.vector.tensor_copy(ks_listed[:], ks_pool[:].indirect(offsets[:]))
-        load_values(3)
+        nb_listed = sb.tile([P, N], F32, name="nb_listed")
+        nc.vector.tensor_copy(nb_listed[:], nb_pool[:].indirect(offsets[:]))
         ks_dealt = sb.tile([P, N], U8, name="ks_dealt", align_bytes=64)
         nc.vector.tensor_copy(
             ks_dealt[:].rearrange("p (t s) -> p s t", t=PACK),
             ks_listed[:].rearrange("p (s t) -> p s t", t=PACK),
         )
-        nb_listed = sb.tile([P, N], F32, name="nb_listed")
-        nc.vector.tensor_copy(nb_listed[:], nb_pool[:].indirect(offsets[:]))
 
-        nb_turned = ps.tile([P, PACK, P], F32, name="nb_turned")
-        for t in range(PACK):
-            nc.tensor.transpose(nb_turned[:, t, :], nb_listed[:, t::PACK], ident[:])
-        bias = sb.tile([P, PACK], F32, name="bias")
-        nc.vector.tensor_tensor(bias[:], nb_turned[:, :, NB_ROW], us_abs[:], MULT)
 
-        q_codes, q_scales = [], []
+        def quantize(woven, words, name, codes=None, scales=None):
+            if codes is None:
+                codes = sb.tile([P, words], U32, name=f"{name}_codes", align_bytes=64)[:]
+                scales = sb.tile([P, words], U8, name=f"{name}_scales", align_bytes=64)[:]
+            nc.vector.quantize_mx(codes.bitcast(FP8X4), scales, woven)
+            return codes, scales
+
+        q_woven = []
         for h in range(HALVES):
-            q_woven = sb.tile([P, QH, PACK], BF16, name=f"q_woven{h}", align_bytes=64)
+            woven = staged_tile([P, QH, PACK], BF16, f"q_woven{h}", f"qw{h}")
             nc.scalar.copy(
-                q_woven[:].rearrange("p (c i) t -> p c t i", i=4),
+                woven[:].rearrange("p (c i) t -> p c t i", i=4),
                 q_raw[:, :, h * QH : (h + 1) * QH].rearrange("p t (c i) -> p c t i", i=4),
             )
-            codes = sb.tile([P, QH], U32, name=f"q_codes{h}", align_bytes=64)
-            scales = sb.tile([P, QH], U8, name=f"q_scales{h}", align_bytes=64)
-            nc.vector.quantize_mx(codes[:].bitcast(FP8X4), scales[:], q_woven[:].rearrange("p q t -> p (q t)"))
-            q_codes.append(codes)
-            q_scales.append(scales)
+            q_woven.append(woven[:].rearrange("p q t -> p (q t)"))
+        nb_dealt = sb.tile([P, PACK, P], F32, name="nb_dealt")
+        nc.scalar.copy(nb_dealt[:], nb_listed[:].rearrange("p (s t) -> p t s", t=PACK))
+        nb_turned = ps.tile([P, PACK, P], F32, name="bank7")
+        for t in range(PACK):
+            nc.tensor.transpose(nb_turned[:, t, :], nb_dealt[:, t, :], ident[:])
+        bias = sb.tile([P, PACK], F32, name="bias")
+        for t in range(PACK):
+            nc.scalar.activation(
+                bias[:, t : t + 1], nb_turned[:, t, NB_ROW : NB_ROW + 1], ACT.Copy, scale=us_abs[:, t : t + 1]
+            )
 
-        y_codes, y_scales = [], []
-        v_codes, v_scales = [], []
+        q_mx = [quantize(q_woven[0], QH, "q0")]
+        kw_listed = staged_tile([P, N], U32, "kw_listed", "c")
+        nc.vector.tensor_copy(kw_listed[:], kw_pool[:].bitcast(U32).indirect(offsets[:]))
+        q_mx.append(quantize(q_woven[1], QH, "q1"))
+        kw_dealt = staged_tile([P, N], U32, "kw_dealt", "qw1")
+        nc.vector.tensor_copy(
+            kw_dealt[:].bitcast(I32).rearrange("p (t s) -> p s t", t=PACK),
+            kw_listed[:].bitcast(I32).rearrange("p (s t) -> p s t", t=PACK),
+        )
+
+        def matmul(acc, lhs, lhs_cols, rhs):
+            nc.tensor.matmul_mx(
+                acc,
+                lhsT=lhs[0][:, lhs_cols].bitcast(FP8X4),
+                lhsT_scale=lhs[1][:, lhs_cols],
+                rhs=rhs[0].bitcast(FP8X4),
+                rhs_scale=rhs[1],
+                start=True,
+                stop=True,
+            )
 
         def first_layer(h):
             pairs = sb.tile([P, 2, QH, 2], BF16, name=f"y_pairs{h}")
             for t in range(PACK):
-                a = ps.tile([P, QH], F32, name=f"bank{t}")
-                nc.tensor.matmul_mx(
-                    a[:],
-                    lhsT=kw_dealt[:, t * P : (t + 1) * P].bitcast(FP8X4),
-                    lhsT_scale=ks_dealt[:, t * P : (t + 1) * P],
-                    rhs=q_codes[h][:].bitcast(FP8X4),
-                    rhs_scale=q_scales[h][:],
-                    start=True,
-                    stop=True,
-                )
+                a = ps.tile([P, QH], F32, name=f"bank{PACK * h + t}")
+                matmul(a[:], (kw_dealt[:], ks_dealt[:]), slice(t * P, (t + 1) * P), q_mx[h])
                 nc.scalar.activation(
                     pairs[:, t // 2, :, t % 2], a[:], ACT.Relu, bias=bias[:, t : t + 1], scale=us_abs[:, t : t + 1]
                 )
-            woven = sb.tile([P, QH, 2, 2], BF16, name=f"y_woven{h}", align_bytes=64)
+            return pairs
+
+        def weave_y(h, pairs, buffer):
+            woven = staged_tile([P, QH, 2, 2], BF16, f"y_woven{h}", buffer)
             nc.vector.tensor_tensor(
                 woven[:],
                 pairs[:].rearrange("p u q e -> p q u e"),
                 us_sign[:].rearrange("p (u e) -> p u e", e=2).unsqueeze(1).to_broadcast([P, QH, 2, 2]),
-                MULT,
+                ALU.mult,
             )
-            codes = sb.tile([P, QH], U32, name=f"y_codes{h}", align_bytes=64)
-            scales = sb.tile([P, QH], U8, name=f"y_scales{h}", align_bytes=64)
-            nc.vector.quantize_mx(codes[:].bitcast(FP8X4), scales[:], woven[:].rearrange("p q u e -> p (q u e)"))
-            y_codes.append(codes)
-            y_scales.append(scales)
+            return quantize(woven[:].rearrange("p q u e -> p (q u e)"), QH, f"y{h}")
 
-        def values(j):
-            listed = sb.tile([P, N], BF16, name=f"v_listed{j}")
-            nc.vector.tensor_copy(listed[:], v_pool[j][:].indirect(offsets[:]))
-            words = listed[:].bitcast(F32)
-            turned = ps.tile([P, 2, P], F32, name=f"v_turned{j % 2}")
-            for u in range(2):
-                nc.tensor.transpose(turned[:, u, :], words[:, u::2], ident[:])
-            woven = sb.tile([P, P * PACK], BF16, name=f"v_woven{j}", align_bytes=64)
-            nc.scalar.copy(
-                woven[:].bitcast(F32).rearrange("p (e u) -> p e u", u=2),
-                turned[:].rearrange("p u e -> p e u"),
+        def gather_values(j, buffer):
+            if isinstance(buffer, (int, str)):
+                listed = staged_tile([P, N], BF16, f"v_listed{j}", buffer)[:]
+            else:
+                listed = buffer
+            nc.vector.tensor_copy(
+                listed.rearrange("p (u s e) -> p s u e", u=2, e=2), v_pool[j][:].indirect(offsets[:])
             )
-            codes = sb.tile([P, P], U32, name=f"v_codes{j}", align_bytes=64)
-            scales = sb.tile([P, P], U8, name=f"v_scales{j}", align_bytes=64)
-            nc.vector.quantize_mx(codes[:].bitcast(FP8X4), scales[:], woven[:])
-            v_codes.append(codes)
-            v_scales.append(scales)
+            return listed
+
+        def turn_values(gathered, bank, buffer):
+            turned = ps.tile([P, len(gathered), 2, P], F32, name=f"bank{bank}")
+            for j, listed in enumerate(gathered):
+                words = listed.bitcast(F32)
+                for u in range(2):
+                    nc.tensor.transpose(turned[:, j, u, :], words[:, u * P : (u + 1) * P], ident[:])
+            woven = staged_tile([P, len(gathered) * P * PACK], BF16, f"v_woven{bank}", buffer)
+            nc.scalar.copy(
+                woven[:].bitcast(F32).rearrange("p (j e u) -> p j e u", e=P, u=2),
+                turned[:].rearrange("p j u e -> p j e u"),
+            )
+            return woven[:]
 
         out_rows = out[0].rearrange("(b p) e -> p b e", p=P)
 
-        def second_layer(j, blocks, bank, copy, queue):
-            o = ps.tile([P, len(blocks), P], F32, name=f"bank{bank}")
-            for n, b in enumerate(blocks):
-                h, c = divmod(b * P, QH)
-                nc.tensor.matmul_mx(
-                    o[:, n, :],
-                    lhsT=y_codes[h][:, c : c + P].bitcast(FP8X4),
-                    lhsT_scale=y_scales[h][:, c : c + P],
-                    rhs=v_codes[j][:].bitcast(FP8X4),
-                    rhs_scale=v_scales[j][:],
-                    start=True,
-                    stop=True,
-                )
-            staged = sb.tile([P, len(blocks), P], F32, name=f"staged{j}_{blocks[0]}")
+        def second_layer(v_mx, e0, width, b0, bank, copy, queue):
+            blocks = 2 if (width == 2 * P or e0 == 3 * P) else 4
+            o = ps.tile([P, blocks, width], F32, name=f"bank{bank}")
+            for n in range(blocks):
+                h, c = divmod((b0 + n) * P, QH)
+                matmul(o[:, n, :], y_mx[h], slice(c, c + P), v_mx)
+            staged = sb.tile([P, blocks, width], F32, name=f"staged{e0}_{b0}")
             copy(staged[:], o[:])
-            queue.dma_start(out_rows[:, blocks[0] : blocks[-1] + 1, j * P : (j + 1) * P], staged[:])
+            queue.dma_start(out_rows[:, b0 : b0 + blocks, e0 : e0 + width], staged[:])
 
-        first_layer(0)
-        values(0)
-        first_layer(1)
-        values(1)
-        second_layer(0, [0, 1, 2, 3], 0, nc.scalar.copy, nc.sync)
-        second_layer(1, [0, 1, 2, 3], 1, nc.scalar.copy, nc.sync)
-        values(2)
-        second_layer(2, [0, 1, 2, 3], 2, nc.scalar.copy, nc.sync)
-        values(3)
-        second_layer(3, [0, 1], 3, nc.scalar.copy, nc.scalar)
-        second_layer(3, [2, 3], 0, nc.vector.tensor_copy, nc.sync)
+        pairs = [first_layer(h) for h in range(HALVES)]
+        v0 = gather_values(0, "c")
+        v1 = gather_values(1, 1)
+        y_mx = [weave_y(0, pairs[0], 2), weave_y(1, pairs[1], "y1")]
+        v01 = turn_values([v0, v1], 5, "f")
+        v01_mx = quantize(v01, 2 * P, "v01")
+        second_layer(v01_mx, 0, 2 * P, 0, 0, nc.scalar.copy, nc.sync)
+        second_layer(v01_mx, 0, 2 * P, 2, 1, nc.scalar.copy, nc.sync)
+        v2 = turn_values([gather_values(2, v01[:, :N])], 6, "w2")
+        v3 = turn_values([gather_values(3, 3)], 7, "w3")
+        v2_codes = staged_tile([P, P], U32, "v2_codes", 4)
+        v2_scales = sb.tile([P, P], U8, name="v2_scales", align_bytes=64)
+        v2_mx = quantize(v2, P, "v2", v2_codes[:], v2_scales[:])
+        second_layer(v2_mx, 2 * P, P, 0, 2, nc.scalar.copy, nc.sync)
+        v3_mx = quantize(v3, P, "v3")
+        second_layer(v3_mx, 3 * P, P, 0, 3, nc.vector.tensor_copy, nc.sync)
+        second_layer(v3_mx, 3 * P, P, 2, 4, nc.scalar.copy, nc.scalar)

@@ -22,6 +22,7 @@ QH = NQ // HALVES
 E_BLOCKS = DV // P
 Q_BLOCKS = NQ // P
 NB_ROW = 16
+NB_SPLIT = 768
 
 
 def tile_attend_mlpb_relu_topk_kernel(tc, qT, k_words, k_scales, vT, nb, us, offs, out):
@@ -40,11 +41,11 @@ def tile_attend_mlpb_relu_topk_kernel(tc, qT, k_words, k_scales, vT, nb, us, off
         nc.sync.dma_start(offsets[:], offs)
         q_raw = staged_tile([P, PACK, NQ], F32, "q_raw", "d")
         nc.sync.dma_start(q_raw[:], qT[0].rearrange("(p t) q -> p t q", t=PACK))
-
         ks_pool = staged_tile([P, T], U8, "ks_pool", "b")
-        nc.vector.memset(ks_pool[:].bitcast(I32), 0)
+        nc.gpsimd.memset(ks_pool[:].bitcast(I32), 0)
         nb_pool = staged_tile([P, T], F32, "nb_pool", "c")
-        nc.vector.memset(nb_pool[:], 0.0)
+        nc.gpsimd.memset(nb_pool[:, :NB_SPLIT], 0.0)
+        nc.vector.memset(nb_pool[:, NB_SPLIT:], 0.0)
         us_col = staged_tile([P, PACK], F32, "us_col", "a")
         nc.scalar.dma_start(us_col[:], us[0].rearrange("(p t) o -> p (t o)", t=PACK))
         for quad in range(4):
@@ -54,7 +55,7 @@ def tile_attend_mlpb_relu_topk_kernel(tc, qT, k_words, k_scales, vT, nb, us, off
             )
         nc.sync.dma_start(nb_pool[NB_ROW : NB_ROW + 1, :], nb[NB_ROW : NB_ROW + 1, :])
 
-        zeros = staged_tile([P, 5 * T], F32, "zeros", 0)
+        zeros = staged_tile([P, (1 + E_BLOCKS) * T], F32, "zeros", 0)
         nc.vector.memset(zeros[:, :P], 0.0)
         ident = sb.tile([P, P], F32, name="ident")
         nc.gpsimd.affine_select(
@@ -70,11 +71,11 @@ def tile_attend_mlpb_relu_topk_kernel(tc, qT, k_words, k_scales, vT, nb, us, off
         nc.sync.dma_start(kw_pool[:], k_words[0].rearrange("p n t -> p (n t)").bitcast(I32))
 
         us_step = sb.tile([P, PACK], F32, name="us_step")
-        nc.vector.tensor_scalar(us_step[:], us_col[:], 0.0, 2.0, ALU.is_ge, ALU.mult)
+        nc.gpsimd.tensor_scalar(us_step[:], us_col[:], 0.0, 2.0, ALU.is_ge, ALU.mult)
         us_sign = sb.tile([P, PACK], BF16, name="us_sign")
-        nc.vector.tensor_scalar(us_sign[:], us_step[:], 1.0, -1.0, ALU.mult, ALU.add)
+        nc.gpsimd.tensor_scalar(us_sign[:], us_step[:], 1.0, -1.0, ALU.mult, ALU.add)
         us_abs = sb.tile([P, PACK], F32, name="us_abs")
-        nc.vector.tensor_tensor(us_abs[:], us_col[:], us_sign[:], ALU.mult)
+        nc.gpsimd.tensor_tensor(us_abs[:], us_col[:], us_sign[:], ALU.mult)
 
         v_pool = []
 
@@ -97,6 +98,9 @@ def tile_attend_mlpb_relu_topk_kernel(tc, qT, k_words, k_scales, vT, nb, us, off
             ks_listed[:].rearrange("p (s t) -> p s t", t=PACK),
         )
 
+        nb_turned = ps.tile([P, PACK, P], F32, name="bank7")
+        for t in range(PACK):
+            nc.tensor.transpose(nb_turned[:, t, :], nb_listed[:, t::PACK], ident[:])
 
         def quantize(woven, words, name, codes=None, scales=None):
             if codes is None:
@@ -113,11 +117,6 @@ def tile_attend_mlpb_relu_topk_kernel(tc, qT, k_words, k_scales, vT, nb, us, off
                 q_raw[:, :, h * QH : (h + 1) * QH].rearrange("p t (c i) -> p c t i", i=4),
             )
             q_woven.append(woven[:].rearrange("p q t -> p (q t)"))
-        nb_dealt = sb.tile([P, PACK, P], F32, name="nb_dealt")
-        nc.scalar.copy(nb_dealt[:], nb_listed[:].rearrange("p (s t) -> p t s", t=PACK))
-        nb_turned = ps.tile([P, PACK, P], F32, name="bank7")
-        for t in range(PACK):
-            nc.tensor.transpose(nb_turned[:, t, :], nb_dealt[:, t, :], ident[:])
         bias = sb.tile([P, PACK], F32, name="bias")
         for t in range(PACK):
             nc.scalar.activation(
@@ -125,10 +124,10 @@ def tile_attend_mlpb_relu_topk_kernel(tc, qT, k_words, k_scales, vT, nb, us, off
             )
 
         q_mx = [quantize(q_woven[0], QH, "q0")]
-        kw_listed = staged_tile([P, N], U32, "kw_listed", "c")
+        kw_listed = staged_tile([P, N], U32, "kw_listed", "kl")
         nc.vector.tensor_copy(kw_listed[:], kw_pool[:].bitcast(U32).indirect(offsets[:]))
         q_mx.append(quantize(q_woven[1], QH, "q1"))
-        kw_dealt = staged_tile([P, N], U32, "kw_dealt", "qw1")
+        kw_dealt = staged_tile([P, N], U32, "kw_dealt", "kd")
         nc.vector.tensor_copy(
             kw_dealt[:].bitcast(I32).rearrange("p (t s) -> p s t", t=PACK),
             kw_listed[:].bitcast(I32).rearrange("p (s t) -> p s t", t=PACK),
@@ -146,7 +145,7 @@ def tile_attend_mlpb_relu_topk_kernel(tc, qT, k_words, k_scales, vT, nb, us, off
             )
 
         def first_layer(h):
-            pairs = sb.tile([P, 2, QH, 2], BF16, name=f"y_pairs{h}")
+            pairs = staged_tile([P, 2, QH, 2], BF16, f"y_pairs{h}", f"pairs{h}")
             for t in range(PACK):
                 a = ps.tile([P, QH], F32, name=f"bank{PACK * h + t}")
                 matmul(a[:], (kw_dealt[:], ks_dealt[:]), slice(t * P, (t + 1) * P), q_mx[h])
@@ -163,16 +162,10 @@ def tile_attend_mlpb_relu_topk_kernel(tc, qT, k_words, k_scales, vT, nb, us, off
                 us_sign[:].rearrange("p (u e) -> p u e", e=2).unsqueeze(1).to_broadcast([P, QH, 2, 2]),
                 ALU.mult,
             )
-            return quantize(woven[:].rearrange("p q u e -> p (q u e)"), QH, f"y{h}")
+            return woven[:].rearrange("p q u e -> p (q u e)")
 
-        def gather_values(j, buffer):
-            if isinstance(buffer, (int, str)):
-                listed = staged_tile([P, N], BF16, f"v_listed{j}", buffer)[:]
-            else:
-                listed = buffer
-            nc.vector.tensor_copy(
-                listed.rearrange("p (u s e) -> p s u e", u=2, e=2), v_pool[j][:].indirect(offsets[:])
-            )
+        def gather_values(j, listed):
+            nc.vector.tensor_copy(listed, v_pool[j][:].indirect(offsets[:]))
             return listed
 
         def turn_values(gathered, bank, buffer):
@@ -180,7 +173,7 @@ def tile_attend_mlpb_relu_topk_kernel(tc, qT, k_words, k_scales, vT, nb, us, off
             for j, listed in enumerate(gathered):
                 words = listed.bitcast(F32)
                 for u in range(2):
-                    nc.tensor.transpose(turned[:, j, u, :], words[:, u * P : (u + 1) * P], ident[:])
+                    nc.tensor.transpose(turned[:, j, u, :], words[:, u::2], ident[:])
             woven = staged_tile([P, len(gathered) * P * PACK], BF16, f"v_woven{bank}", buffer)
             nc.scalar.copy(
                 woven[:].bitcast(F32).rearrange("p (j e u) -> p j e u", e=P, u=2),
@@ -190,30 +183,36 @@ def tile_attend_mlpb_relu_topk_kernel(tc, qT, k_words, k_scales, vT, nb, us, off
 
         out_rows = out[0].rearrange("(b p) e -> p b e", p=P)
 
-        def second_layer(v_mx, e0, width, b0, bank, copy, queue):
+        def second_layer(v_mx, e0, width, b0, bank, copy, queue, buffer=None):
             blocks = 2 if (width == 2 * P or e0 == 3 * P) else 4
             o = ps.tile([P, blocks, width], F32, name=f"bank{bank}")
             for n in range(blocks):
                 h, c = divmod((b0 + n) * P, QH)
                 matmul(o[:, n, :], y_mx[h], slice(c, c + P), v_mx)
-            staged = sb.tile([P, blocks, width], F32, name=f"staged{e0}_{b0}")
+            staged = staged_tile([P, blocks, width], F32, f"staged{e0}_{b0}", buffer or f"staged{e0}_{b0}")
             copy(staged[:], o[:])
             queue.dma_start(out_rows[:, b0 : b0 + blocks, e0 : e0 + width], staged[:])
 
         pairs = [first_layer(h) for h in range(HALVES)]
-        v0 = gather_values(0, "c")
-        v1 = gather_values(1, 1)
-        y_mx = [weave_y(0, pairs[0], 2), weave_y(1, pairs[1], "y1")]
-        v01 = turn_values([v0, v1], 5, "f")
-        v01_mx = quantize(v01, 2 * P, "v01")
+        listed01 = staged_tile([P, 2 * N], BF16, "v_listed01", "kl")
+        v0 = gather_values(0, listed01[:, :N])
+        v1 = gather_values(1, listed01[:, N:])
+        y_mx = [quantize(weave_y(0, pairs[0], 2), QH, "y0")]
+        woven01 = turn_values([v0, v1], 5, "w01")
+        v2 = gather_values(2, staged_tile([P, N], BF16, "v_listed2", "pairs0")[:])
+        woven2 = turn_values([v2], 6, "w2")
+        y_woven1 = weave_y(1, pairs[1], 3)
+        v01_codes = staged_tile([P, 2 * P], U32, "v01_codes", "pairs1")
+        v01_scales = sb.tile([P, 2 * P], U8, name="v01_scales", align_bytes=64)
+        v01_mx = quantize(woven01, 2 * P, "v01", v01_codes[:], v01_scales[:])
+        y_mx.append(quantize(y_woven1, QH, "y1"))
+        v2_codes = staged_tile([P, P], U32, "v2_codes", "w01")
+        v2_scales = sb.tile([P, P], U8, name="v2_scales", align_bytes=64)
+        v2_mx = quantize(woven2, P, "v2", v2_codes[:], v2_scales[:])
         second_layer(v01_mx, 0, 2 * P, 0, 0, nc.scalar.copy, nc.sync)
         second_layer(v01_mx, 0, 2 * P, 2, 1, nc.scalar.copy, nc.sync)
-        v2 = turn_values([gather_values(2, v01[:, :N])], 6, "w2")
-        v3 = turn_values([gather_values(3, 3)], 7, "w3")
-        v2_codes = staged_tile([P, P], U32, "v2_codes", 4)
-        v2_scales = sb.tile([P, P], U8, name="v2_scales", align_bytes=64)
-        v2_mx = quantize(v2, P, "v2", v2_codes[:], v2_scales[:])
-        second_layer(v2_mx, 2 * P, P, 0, 2, nc.scalar.copy, nc.sync)
-        v3_mx = quantize(v3, P, "v3")
+        v3 = gather_values(3, woven2)
+        second_layer(v2_mx, 2 * P, P, 0, 2, nc.vector.tensor_copy, nc.sync, 4)
+        v3_mx = quantize(turn_values([v3], 7, "w3"), P, "v3")
         second_layer(v3_mx, 3 * P, P, 0, 3, nc.vector.tensor_copy, nc.sync)
         second_layer(v3_mx, 3 * P, P, 2, 4, nc.scalar.copy, nc.scalar)

@@ -22,7 +22,6 @@ QH = NQ // HALVES
 E_BLOCKS = DV // P
 Q_BLOCKS = NQ // P
 NB_ROW = 16
-NB_SPLIT = 768
 
 
 def tile_attend_mlpb_relu_topk_kernel(tc, qT, k_words, k_scales, vT, nb, us, offs, out):
@@ -39,13 +38,14 @@ def tile_attend_mlpb_relu_topk_kernel(tc, qT, k_words, k_scales, vT, nb, us, off
 
         offsets = sb.tile([P, N // 16], U16, name="offsets")
         nc.sync.dma_start(offsets[:], offs)
+        kw_pool = staged_tile([P, T], I32, "kw_pool", "e")
+        nc.sync.dma_start(kw_pool[:], k_words[0].rearrange("p n t -> p (n t)").bitcast(I32))
         q_raw = staged_tile([P, PACK, NQ], F32, "q_raw", "d")
         nc.sync.dma_start(q_raw[:], qT[0].rearrange("(p t) q -> p t q", t=PACK))
         ks_pool = staged_tile([P, T], U8, "ks_pool", "b")
         nc.gpsimd.memset(ks_pool[:].bitcast(I32), 0)
         nb_pool = staged_tile([P, T], F32, "nb_pool", "c")
-        nc.gpsimd.memset(nb_pool[:, :NB_SPLIT], 0.0)
-        nc.vector.memset(nb_pool[:, NB_SPLIT:], 0.0)
+        nc.vector.memset(nb_pool[:], 0.0)
         us_col = staged_tile([P, PACK], F32, "us_col", "a")
         nc.scalar.dma_start(us_col[:], us[0].rearrange("(p t) o -> p (t o)", t=PACK))
         for quad in range(4):
@@ -53,9 +53,9 @@ def tile_attend_mlpb_relu_topk_kernel(tc, qT, k_words, k_scales, vT, nb, us, off
                 ks_pool[32 * quad : 32 * quad + 4, :].bitcast(I32),
                 k_scales[0][4 * quad : 4 * quad + 4, :].bitcast(I32),
             )
-        nc.sync.dma_start(nb_pool[NB_ROW : NB_ROW + 1, :], nb[NB_ROW : NB_ROW + 1, :])
+        nc.scalar.dma_start(nb_pool[NB_ROW : NB_ROW + 1, :], nb[NB_ROW : NB_ROW + 1, :])
 
-        zeros = staged_tile([P, (1 + E_BLOCKS) * T], F32, "zeros", 0)
+        zeros = staged_tile([P, E_BLOCKS * T], F32, "zeros", 0)
         nc.vector.memset(zeros[:, :P], 0.0)
         ident = sb.tile([P, P], F32, name="ident")
         nc.gpsimd.affine_select(
@@ -67,8 +67,6 @@ def tile_attend_mlpb_relu_topk_kernel(tc, qT, k_words, k_scales, vT, nb, us, off
             pattern=[[-1, P]],
             channel_multiplier=1,
         )
-        kw_pool = staged_tile([P, T], I32, "kw_pool", 0)
-        nc.sync.dma_start(kw_pool[:], k_words[0].rearrange("p n t -> p (n t)").bitcast(I32))
 
         us_step = sb.tile([P, PACK], F32, name="us_step")
         nc.gpsimd.tensor_scalar(us_step[:], us_col[:], 0.0, 2.0, ALU.is_ge, ALU.mult)
@@ -86,16 +84,23 @@ def tile_attend_mlpb_relu_topk_kernel(tc, qT, k_words, k_scales, vT, nb, us, off
             v_pool.append(v_tile)
 
         for j in range(E_BLOCKS):
-            load_values(1 + j)
+            load_values(j)
 
+        kw_listed = staged_tile([P, N], U32, "kw_listed", "kl")
+        nc.vector.tensor_copy(kw_listed[:], kw_pool[:].bitcast(U32).indirect(offsets[:]))
+        kw_dealt = sb.tile([P, N], U32, name="kw_dealt", align_bytes=64)
+        nc.vector.tensor_copy(
+            kw_dealt[:].bitcast(I32).rearrange("p (t c i) -> p c t i", t=PACK, i=4),
+            kw_listed[:].bitcast(I32).rearrange("p (c i t) -> p c t i", t=PACK, i=4),
+        )
         ks_listed = sb.tile([P, N], U8, name="ks_listed")
         nc.vector.tensor_copy(ks_listed[:], ks_pool[:].indirect(offsets[:]))
         nb_listed = sb.tile([P, N], F32, name="nb_listed")
         nc.vector.tensor_copy(nb_listed[:], nb_pool[:].indirect(offsets[:]))
         ks_dealt = sb.tile([P, N], U8, name="ks_dealt", align_bytes=64)
         nc.vector.tensor_copy(
-            ks_dealt[:].rearrange("p (t s) -> p s t", t=PACK),
-            ks_listed[:].rearrange("p (s t) -> p s t", t=PACK),
+            ks_dealt[:].rearrange("p (t c i) -> p c t i", t=PACK, i=16),
+            ks_listed[:].rearrange("p (c i t) -> p c t i", t=PACK, i=16),
         )
 
         nb_turned = ps.tile([P, PACK, P], F32, name="bank7")
@@ -124,14 +129,7 @@ def tile_attend_mlpb_relu_topk_kernel(tc, qT, k_words, k_scales, vT, nb, us, off
             )
 
         q_mx = [quantize(q_woven[0], QH, "q0")]
-        kw_listed = staged_tile([P, N], U32, "kw_listed", "kl")
-        nc.vector.tensor_copy(kw_listed[:], kw_pool[:].bitcast(U32).indirect(offsets[:]))
         q_mx.append(quantize(q_woven[1], QH, "q1"))
-        kw_dealt = staged_tile([P, N], U32, "kw_dealt", "kd")
-        nc.vector.tensor_copy(
-            kw_dealt[:].bitcast(I32).rearrange("p (t s) -> p s t", t=PACK),
-            kw_listed[:].bitcast(I32).rearrange("p (s t) -> p s t", t=PACK),
-        )
 
         def matmul(acc, lhs, lhs_cols, rhs):
             nc.tensor.matmul_mx(
@@ -194,14 +192,14 @@ def tile_attend_mlpb_relu_topk_kernel(tc, qT, k_words, k_scales, vT, nb, us, off
             queue.dma_start(out_rows[:, b0 : b0 + blocks, e0 : e0 + width], staged[:])
 
         pairs = [first_layer(h) for h in range(HALVES)]
-        listed01 = staged_tile([P, 2 * N], BF16, "v_listed01", "kl")
+        listed01 = staged_tile([P, 2 * N], BF16, "v_listed01", "qw1")
         v0 = gather_values(0, listed01[:, :N])
         v1 = gather_values(1, listed01[:, N:])
-        y_mx = [quantize(weave_y(0, pairs[0], 2), QH, "y0")]
+        y_mx = [quantize(weave_y(0, pairs[0], 1), QH, "y0")]
         woven01 = turn_values([v0, v1], 5, "w01")
         v2 = gather_values(2, staged_tile([P, N], BF16, "v_listed2", "pairs0")[:])
         woven2 = turn_values([v2], 6, "w2")
-        y_woven1 = weave_y(1, pairs[1], 3)
+        y_woven1 = weave_y(1, pairs[1], 2)
         v01_codes = staged_tile([P, 2 * P], U32, "v01_codes", "pairs1")
         v01_scales = sb.tile([P, 2 * P], U8, name="v01_scales", align_bytes=64)
         v01_mx = quantize(woven01, 2 * P, "v01", v01_codes[:], v01_scales[:])
@@ -212,7 +210,7 @@ def tile_attend_mlpb_relu_topk_kernel(tc, qT, k_words, k_scales, vT, nb, us, off
         second_layer(v01_mx, 0, 2 * P, 0, 0, nc.scalar.copy, nc.sync)
         second_layer(v01_mx, 0, 2 * P, 2, 1, nc.scalar.copy, nc.sync)
         v3 = gather_values(3, woven2)
-        second_layer(v2_mx, 2 * P, P, 0, 2, nc.vector.tensor_copy, nc.sync, 4)
+        second_layer(v2_mx, 2 * P, P, 0, 2, nc.vector.tensor_copy, nc.sync, 3)
         v3_mx = quantize(turn_values([v3], 7, "w3"), P, "v3")
         second_layer(v3_mx, 3 * P, P, 0, 3, nc.vector.tensor_copy, nc.sync)
         second_layer(v3_mx, 3 * P, P, 2, 4, nc.scalar.copy, nc.scalar)

@@ -4,6 +4,7 @@ import concourse.mybir as mybir
 
 T, D, NQ, N, DV = 2048, 512, 512, 512, 512
 FLOPS = 2 * N * D * NQ + 2 * NQ * N * DV
+BYTES = 4 * D * NQ + D * T + D // 32 * T + 4 * DV * T + 4 * T + 4 * N + 128 * (N // 16) * 2 + 4 * NQ * DV
 
 F32 = mybir.dt.float32
 BF16 = mybir.dt.bfloat16
@@ -17,47 +18,74 @@ ALU = mybir.AluOpType
 
 P = 128
 PACK = 4
-HALVES = 2
-QH = NQ // HALVES
+QH = NQ // 2
 E_BLOCKS = DV // P
-Q_BLOCKS = NQ // P
+TABLE_BYTES = T * 4
 NB_ROW = 16
+NB_SHARE = 768
+MX_ALIGN = 64
 
 
 def tile_attend_mlpb_relu_topk_kernel(tc, qT, k_words, k_scales, vT, nb, us, offs, out):
     nc = tc.nc
     with ExitStack() as ctx:
         sb = ctx.enter_context(tc.tile_pool(name="sb", bufs=1))
-        area = ctx.enter_context(tc.tile_pool(name="area", bufs=1))
+        tables = ctx.enter_context(tc.tile_pool(name="tables", bufs=1))
+        bias_area = ctx.enter_context(tc.tile_pool(name="bias_area", bufs=1))
         ps = ctx.enter_context(tc.psum_pool(name="ps", bufs=1))
 
-        def staged_tile(shape, dtype, name, buffer):
-            if isinstance(buffer, int):
-                return area.tile(shape, dtype, name=name, offset=buffer * T * 4, align_bytes=64)
-            return sb.tile(shape, dtype, name=name, tag=buffer, align_bytes=64)
+        def own(shape, dtype, name):
+            return sb.tile(shape, dtype, name=name, align_bytes=MX_ALIGN)
+
+        def after(former, shape, dtype, name):
+            return sb.tile(shape, dtype, name=name, tag=former, align_bytes=MX_ALIGN)
+
+        def on_table(slot, shape, dtype, name):
+            return tables.tile(shape, dtype, name=name, offset=slot * TABLE_BYTES, align_bytes=MX_ALIGN)
+
+        def on_nb(offset, shape, dtype, name):
+            return bias_area.tile(shape, dtype, name=name, offset=offset, align_bytes=MX_ALIGN)
+
+        def bank(index, shape):
+            return ps.tile(shape, F32, name=f"bank{index}")
+
+        def quantize(woven, codes, scales):
+            nc.vector.quantize_mx(codes[:].bitcast(FP8X4), scales[:], woven)
+            return codes, scales
+
+        def matmul(acc, stationary, stationary_cols, moving, moving_cols):
+            nc.tensor.matmul_mx(
+                acc,
+                lhsT=stationary[0][:, stationary_cols].bitcast(FP8X4),
+                lhsT_scale=stationary[1][:, stationary_cols],
+                rhs=moving[0][:, moving_cols].bitcast(FP8X4),
+                rhs_scale=moving[1][:, moving_cols],
+                start=True,
+                stop=True,
+            )
 
         offsets = sb.tile([P, N // 16], U16, name="offsets")
         nc.sync.dma_start(offsets[:], offs)
-        kw_pool = staged_tile([P, T], I32, "kw_pool", "e")
-        nc.sync.dma_start(kw_pool[:], k_words[0].rearrange("p n t -> p (n t)").bitcast(I32))
-        q_raw = staged_tile([P, PACK, NQ], F32, "q_raw", "d")
+        q_raw = own([P, PACK, NQ], F32, "q_raw")
         nc.sync.dma_start(q_raw[:], qT[0].rearrange("(p t) q -> p t q", t=PACK))
-        ks_pool = staged_tile([P, T], U8, "ks_pool", "b")
-        nc.gpsimd.memset(ks_pool[:].bitcast(I32), 0)
-        nb_pool = staged_tile([P, T], F32, "nb_pool", "c")
-        nc.vector.memset(nb_pool[:], 0.0)
-        us_col = staged_tile([P, PACK], F32, "us_col", "a")
+
+        ks_table = own([P, T], U8, "ks_table")
+        nc.gpsimd.memset(ks_table[:].bitcast(I32), 0)
+        nb_table = on_nb(0, [P, T], F32, "nb_table")
+        nc.gpsimd.memset(nb_table[:, :NB_SHARE], 0.0)
+        nc.vector.memset(nb_table[:, NB_SHARE:], 0.0)
+        us_col = own([P, PACK], F32, "us_col")
         nc.scalar.dma_start(us_col[:], us[0].rearrange("(p t) o -> p (t o)", t=PACK))
         for quad in range(4):
             nc.scalar.dma_start(
-                ks_pool[32 * quad : 32 * quad + 4, :].bitcast(I32),
+                ks_table[32 * quad : 32 * quad + 4, :].bitcast(I32),
                 k_scales[0][4 * quad : 4 * quad + 4, :].bitcast(I32),
             )
-        nc.scalar.dma_start(nb_pool[NB_ROW : NB_ROW + 1, :], nb[NB_ROW : NB_ROW + 1, :])
+        nc.scalar.dma_start(nb_table[NB_ROW : NB_ROW + 1, :], nb[NB_ROW : NB_ROW + 1, :])
 
-        zeros = staged_tile([P, E_BLOCKS * T], F32, "zeros", 0)
+        zeros = on_table(0, [P, (1 + E_BLOCKS) * T], F32, "zeros")
         nc.vector.memset(zeros[:, :P], 0.0)
-        ident = sb.tile([P, P], F32, name="ident")
+        ident = own([P, P], F32, "ident")
         nc.gpsimd.affine_select(
             out=ident[:],
             in_=zeros[:, :P],
@@ -67,93 +95,67 @@ def tile_attend_mlpb_relu_topk_kernel(tc, qT, k_words, k_scales, vT, nb, us, off
             pattern=[[-1, P]],
             channel_multiplier=1,
         )
+        kw_table = on_table(0, [P, T], I32, "kw_table")
+        nc.sync.dma_start(kw_table[:], k_words[0].rearrange("p n t -> p (n t)").bitcast(I32))
+        v_tables = []
+        for j in range(E_BLOCKS):
+            v_table = on_table(1 + j, [P, T], F32, f"v_table{j}")
+            nc.sync.dma_start(v_table[:], vT[j * P : (j + 1) * P, :])
+            v_tables.append(v_table)
 
-        us_step = sb.tile([P, PACK], F32, name="us_step")
+        us_step = own([P, PACK], F32, "us_step")
         nc.gpsimd.tensor_scalar(us_step[:], us_col[:], 0.0, 2.0, ALU.is_ge, ALU.mult)
-        us_sign = sb.tile([P, PACK], BF16, name="us_sign")
+        us_sign = own([P, PACK], BF16, "us_sign")
         nc.gpsimd.tensor_scalar(us_sign[:], us_step[:], 1.0, -1.0, ALU.mult, ALU.add)
-        us_abs = sb.tile([P, PACK], F32, name="us_abs")
+        us_abs = own([P, PACK], F32, "us_abs")
         nc.gpsimd.tensor_tensor(us_abs[:], us_col[:], us_sign[:], ALU.mult)
 
-        v_pool = []
-
-        def load_values(buffer):
-            j = len(v_pool)
-            v_tile = staged_tile([P, T], F32, f"v_pool{j}", buffer)
-            nc.sync.dma_start(v_tile[:], vT[j * P : (j + 1) * P, :])
-            v_pool.append(v_tile)
-
-        for j in range(E_BLOCKS):
-            load_values(j)
-
-        kw_listed = staged_tile([P, N], U32, "kw_listed", "kl")
-        nc.vector.tensor_copy(kw_listed[:], kw_pool[:].bitcast(U32).indirect(offsets[:]))
-        kw_dealt = sb.tile([P, N], U32, name="kw_dealt", align_bytes=64)
-        nc.vector.tensor_copy(
-            kw_dealt[:].bitcast(I32).rearrange("p (t c i) -> p c t i", t=PACK, i=4),
-            kw_listed[:].bitcast(I32).rearrange("p (c i t) -> p c t i", t=PACK, i=4),
-        )
-        ks_listed = sb.tile([P, N], U8, name="ks_listed")
-        nc.vector.tensor_copy(ks_listed[:], ks_pool[:].indirect(offsets[:]))
-        nb_listed = sb.tile([P, N], F32, name="nb_listed")
-        nc.vector.tensor_copy(nb_listed[:], nb_pool[:].indirect(offsets[:]))
-        ks_dealt = sb.tile([P, N], U8, name="ks_dealt", align_bytes=64)
+        ks_listed = own([P, N], U8, "ks_listed")
+        nc.vector.tensor_copy(ks_listed[:], ks_table[:].indirect(offsets[:]))
+        nb_listed = own([P, N], F32, "nb_listed")
+        nc.vector.tensor_copy(nb_listed[:], nb_table[:].indirect(offsets[:]))
+        ks_dealt = on_nb(0, [P, N], U8, "ks_dealt")
         nc.vector.tensor_copy(
             ks_dealt[:].rearrange("p (t c i) -> p c t i", t=PACK, i=16),
             ks_listed[:].rearrange("p (c i t) -> p c t i", t=PACK, i=16),
         )
 
-        nb_turned = ps.tile([P, PACK, P], F32, name="bank7")
+        q_woven = own([P, NQ, PACK], BF16, "q_woven")
+        nc.scalar.copy(
+            q_woven[:].rearrange("p (c i) t -> p c t i", i=4),
+            q_raw[:].rearrange("p t (c i) -> p c t i", i=4),
+        )
+        q_mx = quantize(
+            q_woven[:].rearrange("p q t -> p (q t)"),
+            on_nb(N, [P, NQ], U32, "q_codes"),
+            own([P, NQ], U8, "q_scales"),
+        )
+        kw_dealt = on_nb(N + NQ * 4, [P, N], U32, "kw_dealt")
+        nc.vector.tensor_copy(
+            kw_dealt[:].rearrange("p (t s) -> p s t", t=PACK),
+            kw_table[:].bitcast(U32).indirect(offsets[:]),
+        )
+
+        nb_turned = bank(7, [P, PACK, P])
         for t in range(PACK):
             nc.tensor.transpose(nb_turned[:, t, :], nb_listed[:, t::PACK], ident[:])
-
-        def quantize(woven, words, name, codes=None, scales=None):
-            if codes is None:
-                codes = sb.tile([P, words], U32, name=f"{name}_codes", align_bytes=64)[:]
-                scales = sb.tile([P, words], U8, name=f"{name}_scales", align_bytes=64)[:]
-            nc.vector.quantize_mx(codes.bitcast(FP8X4), scales, woven)
-            return codes, scales
-
-        q_woven = []
-        for h in range(HALVES):
-            woven = staged_tile([P, QH, PACK], BF16, f"q_woven{h}", f"qw{h}")
-            nc.scalar.copy(
-                woven[:].rearrange("p (c i) t -> p c t i", i=4),
-                q_raw[:, :, h * QH : (h + 1) * QH].rearrange("p t (c i) -> p c t i", i=4),
-            )
-            q_woven.append(woven[:].rearrange("p q t -> p (q t)"))
-        bias = sb.tile([P, PACK], F32, name="bias")
+        bias = own([P, PACK], F32, "bias")
         for t in range(PACK):
             nc.scalar.activation(
                 bias[:, t : t + 1], nb_turned[:, t, NB_ROW : NB_ROW + 1], ACT.Copy, scale=us_abs[:, t : t + 1]
             )
 
-        q_mx = [quantize(q_woven[0], QH, "q0")]
-        q_mx.append(quantize(q_woven[1], QH, "q1"))
-
-        def matmul(acc, lhs, lhs_cols, rhs):
-            nc.tensor.matmul_mx(
-                acc,
-                lhsT=lhs[0][:, lhs_cols].bitcast(FP8X4),
-                lhsT_scale=lhs[1][:, lhs_cols],
-                rhs=rhs[0].bitcast(FP8X4),
-                rhs_scale=rhs[1],
-                start=True,
-                stop=True,
-            )
-
         def first_layer(h):
-            pairs = staged_tile([P, 2, QH, 2], BF16, f"y_pairs{h}", f"pairs{h}")
+            pairs = own([P, 2, QH, 2], BF16, f"y_pairs{h}")
             for t in range(PACK):
-                a = ps.tile([P, QH], F32, name=f"bank{PACK * h + t}")
-                matmul(a[:], (kw_dealt[:], ks_dealt[:]), slice(t * P, (t + 1) * P), q_mx[h])
+                a = bank(PACK * h + t, [P, QH])
+                matmul(a[:], (kw_dealt, ks_dealt), slice(t * P, (t + 1) * P), q_mx, slice(h * QH, (h + 1) * QH))
                 nc.scalar.activation(
                     pairs[:, t // 2, :, t % 2], a[:], ACT.Relu, bias=bias[:, t : t + 1], scale=us_abs[:, t : t + 1]
                 )
             return pairs
 
-        def weave_y(h, pairs, buffer):
-            woven = staged_tile([P, QH, 2, 2], BF16, f"y_woven{h}", buffer)
+        def weave_y(pairs, woven):
             nc.vector.tensor_tensor(
                 woven[:],
                 pairs[:].rearrange("p u q e -> p q u e"),
@@ -163,16 +165,15 @@ def tile_attend_mlpb_relu_topk_kernel(tc, qT, k_words, k_scales, vT, nb, us, off
             return woven[:].rearrange("p q u e -> p (q u e)")
 
         def gather_values(j, listed):
-            nc.vector.tensor_copy(listed, v_pool[j][:].indirect(offsets[:]))
+            nc.vector.tensor_copy(listed, v_tables[j][:].indirect(offsets[:]))
             return listed
 
-        def turn_values(gathered, bank, buffer):
-            turned = ps.tile([P, len(gathered), 2, P], F32, name=f"bank{bank}")
+        def turn_values(gathered, bank_index, name):
+            turned = bank(bank_index, [P, len(gathered), 2, P])
             for j, listed in enumerate(gathered):
-                words = listed.bitcast(F32)
                 for u in range(2):
-                    nc.tensor.transpose(turned[:, j, u, :], words[:, u::2], ident[:])
-            woven = staged_tile([P, len(gathered) * P * PACK], BF16, f"v_woven{bank}", buffer)
+                    nc.tensor.transpose(turned[:, j, u, :], listed.bitcast(F32)[:, u::2], ident[:])
+            woven = own([P, len(gathered) * P * PACK], BF16, name)
             nc.scalar.copy(
                 woven[:].bitcast(F32).rearrange("p (j e u) -> p j e u", e=P, u=2),
                 turned[:].rearrange("p j u e -> p j e u"),
@@ -180,37 +181,39 @@ def tile_attend_mlpb_relu_topk_kernel(tc, qT, k_words, k_scales, vT, nb, us, off
             return woven[:]
 
         out_rows = out[0].rearrange("(b p) e -> p b e", p=P)
+        y_mx = []
 
-        def second_layer(v_mx, e0, width, b0, bank, copy, queue, buffer=None):
-            blocks = 2 if (width == 2 * P or e0 == 3 * P) else 4
-            o = ps.tile([P, blocks, width], F32, name=f"bank{bank}")
-            for n in range(blocks):
-                h, c = divmod((b0 + n) * P, QH)
-                matmul(o[:, n, :], y_mx[h], slice(c, c + P), v_mx)
-            staged = staged_tile([P, blocks, width], F32, f"staged{e0}_{b0}", buffer or f"staged{e0}_{b0}")
-            copy(staged[:], o[:])
-            queue.dma_start(out_rows[:, b0 : b0 + blocks, e0 : e0 + width], staged[:])
+        def second_layer(v_mx, e0, q_blocks, bank_index, staged, copy, queue):
+            width = v_mx[1].shape[1]
+            acc = bank(bank_index, [P, len(q_blocks), width])
+            for n, b in enumerate(q_blocks):
+                h, c = divmod(b * P, QH)
+                matmul(acc[:, n, :], y_mx[h], slice(c, c + P), v_mx, slice(0, width))
+            copy(staged[:], acc[:])
+            queue.dma_start(out_rows[:, q_blocks.start : q_blocks.stop, e0 : e0 + width], staged[:])
 
-        pairs = [first_layer(h) for h in range(HALVES)]
-        listed01 = staged_tile([P, 2 * N], BF16, "v_listed01", "qw1")
+        pairs = [first_layer(h) for h in range(2)]
+        listed01 = after("q_woven", [P, 2 * N], BF16, "v_listed01")
         v0 = gather_values(0, listed01[:, :N])
         v1 = gather_values(1, listed01[:, N:])
-        y_mx = [quantize(weave_y(0, pairs[0], 1), QH, "y0")]
-        woven01 = turn_values([v0, v1], 5, "w01")
-        v2 = gather_values(2, staged_tile([P, N], BF16, "v_listed2", "pairs0")[:])
-        woven2 = turn_values([v2], 6, "w2")
-        y_woven1 = weave_y(1, pairs[1], 2)
-        v01_codes = staged_tile([P, 2 * P], U32, "v01_codes", "pairs1")
-        v01_scales = sb.tile([P, 2 * P], U8, name="v01_scales", align_bytes=64)
-        v01_mx = quantize(woven01, 2 * P, "v01", v01_codes[:], v01_scales[:])
-        y_mx.append(quantize(y_woven1, QH, "y1"))
-        v2_codes = staged_tile([P, P], U32, "v2_codes", "w01")
-        v2_scales = sb.tile([P, P], U8, name="v2_scales", align_bytes=64)
-        v2_mx = quantize(woven2, P, "v2", v2_codes[:], v2_scales[:])
-        second_layer(v01_mx, 0, 2 * P, 0, 0, nc.scalar.copy, nc.sync)
-        second_layer(v01_mx, 0, 2 * P, 2, 1, nc.scalar.copy, nc.sync)
-        v3 = gather_values(3, woven2)
-        second_layer(v2_mx, 2 * P, P, 0, 2, nc.vector.tensor_copy, nc.sync, 3)
-        v3_mx = quantize(turn_values([v3], 7, "w3"), P, "v3")
-        second_layer(v3_mx, 3 * P, P, 0, 3, nc.vector.tensor_copy, nc.sync)
-        second_layer(v3_mx, 3 * P, P, 2, 4, nc.scalar.copy, nc.scalar)
+        y_woven0 = weave_y(pairs[0], on_table(2, [P, QH, 2, 2], BF16, "y_woven0"))
+        y_mx.append(quantize(y_woven0, own([P, QH], U32, "y0_codes"), own([P, QH], U8, "y0_scales")))
+        v_woven01 = turn_values([v0, v1], 5, "v_woven01")
+        v2 = gather_values(2, after("y_pairs0", [P, N], BF16, "v_listed2")[:])
+        v_woven2 = turn_values([v2], 6, "v_woven2")
+        y_woven1 = weave_y(pairs[1], on_table(3, [P, QH, 2, 2], BF16, "y_woven1"))
+        v01_mx = quantize(
+            v_woven01, after("y_pairs1", [P, 2 * P], U32, "v01_codes"), own([P, 2 * P], U8, "v01_scales")
+        )
+        y_mx.append(quantize(y_woven1, own([P, QH], U32, "y1_codes"), own([P, QH], U8, "y1_scales")))
+        v2_mx = quantize(v_woven2, after("v_woven01", [P, P], U32, "v2_codes"), own([P, P], U8, "v2_scales"))
+        for half in range(2):
+            staged = own([P, 2, 2 * P], F32, f"staged01_{half}")
+            second_layer(v01_mx, 0, range(2 * half, 2 * half + 2), half, staged, nc.scalar.copy, nc.sync)
+        v3 = gather_values(3, v_woven2)
+        staged2 = on_table(4, [P, 4, P], F32, "staged2")
+        second_layer(v2_mx, 2 * P, range(4), 2, staged2, nc.vector.tensor_copy, nc.sync)
+        v_woven3 = turn_values([v3], 7, "v_woven3")
+        v3_mx = quantize(v_woven3, own([P, P], U32, "v3_codes"), own([P, P], U8, "v3_scales"))
+        second_layer(v3_mx, 3 * P, range(0, 2), 3, own([P, 2, P], F32, "staged3_0"), nc.vector.tensor_copy, nc.sync)
+        second_layer(v3_mx, 3 * P, range(2, 4), 4, own([P, 2, P], F32, "staged3_1"), nc.scalar.copy, nc.scalar)

from contextlib import ExitStack

import concourse.mybir as mybir

T, D, NQ, N, DV = 2048, 512, 512, 512, 512
FLOPS = 2 * N * D * NQ + 2 * NQ * N * DV
BYTES = 4 * D * NQ + D * T + D // 32 * T + 4 * DV * T + 4 * T + 4 * N + 128 * (N // 16) * 2 + 4 * NQ * DV

F32 = mybir.dt.float32
BF16 = mybir.dt.bfloat16
I32 = mybir.dt.int32
U32 = mybir.dt.uint32
U16 = mybir.dt.uint16
U8 = mybir.dt.uint8
FP8X4 = mybir.dt.float8_e4m3fn_x4
ACT = mybir.ActivationFunctionType
ALU = mybir.AluOpType

P = 128
PACK = 4
QH = NQ // 2
E_BLOCKS = DV // P
TABLE_BYTES = T * 4
NB_ROW = 16
NB_SHARE = 768
MX_ALIGN = 64


def tile_attend_mlpb_relu_topk_kernel(tc, qT, k_words, k_scales, vT, nb, us, offs, out):
    nc = tc.nc
    with ExitStack() as ctx:
        sb = ctx.enter_context(tc.tile_pool(name="sb", bufs=1))
        tables = ctx.enter_context(tc.tile_pool(name="tables", bufs=1))
        bias_area = ctx.enter_context(tc.tile_pool(name="bias_area", bufs=1))
        ps = ctx.enter_context(tc.psum_pool(name="ps", bufs=1))

        def own(shape, dtype, name):
            return sb.tile(shape, dtype, name=name, align_bytes=MX_ALIGN)

        def after(former, shape, dtype, name):
            return sb.tile(shape, dtype, name=name, tag=former, align_bytes=MX_ALIGN)

        def on_table(slot, shape, dtype, name):
            return tables.tile(shape, dtype, name=name, offset=slot * TABLE_BYTES, align_bytes=MX_ALIGN)

        def on_nb(offset, shape, dtype, name):
            return bias_area.tile(shape, dtype, name=name, offset=offset, align_bytes=MX_ALIGN)

        def bank(index, shape):
            return ps.tile(shape, F32, name=f"bank{index}")

        def quantize(woven, codes, scales):
            nc.vector.quantize_mx(codes[:].bitcast(FP8X4), scales[:], woven)
            return codes, scales

        def matmul(acc, stationary, stationary_cols, moving, moving_cols):
            nc.tensor.matmul_mx(
                acc,
                lhsT=stationary[0][:, stationary_cols].bitcast(FP8X4),
                lhsT_scale=stationary[1][:, stationary_cols],
                rhs=moving[0][:, moving_cols].bitcast(FP8X4),
                rhs_scale=moving[1][:, moving_cols],
                start=True,
                stop=True,
            )

        offsets = sb.tile([P, N // 16], U16, name="offsets")
        nc.sync.dma_start(offsets[:], offs)
        q_raw = own([P, PACK, NQ], F32, "q_raw")
        nc.sync.dma_start(q_raw[:], qT[0].rearrange("(p t) q -> p t q", t=PACK))

        ks_table = own([P, T], U8, "ks_table")
        nc.gpsimd.memset(ks_table[:].bitcast(I32), 0)
        nb_table = on_nb(0, [P, T], F32, "nb_table")
        nc.gpsimd.memset(nb_table[:, :NB_SHARE], 0.0)
        nc.vector.memset(nb_table[:, NB_SHARE:], 0.0)
        us_col = own([P, PACK], F32, "us_col")
        nc.scalar.dma_start(us_col[:], us[0].rearrange("(p t) o -> p (t o)", t=PACK))
        for quad in range(4):
            nc.scalar.dma_start(
                ks_table[32 * quad : 32 * quad + 4, :].bitcast(I32),
                k_scales[0][4 * quad : 4 * quad + 4, :].bitcast(I32),
            )
        nc.scalar.dma_start(nb_table[NB_ROW : NB_ROW + 1, :], nb[NB_ROW : NB_ROW + 1, :])

        zeros = on_table(0, [P, (1 + E_BLOCKS) * T], F32, "zeros")
        nc.vector.memset(zeros[:, :P], 0.0)
        ident = own([P, P], F32, "ident")
        nc.gpsimd.affine_select(
            out=ident[:],
            in_=zeros[:, :P],
            compare_op=ALU.not_equal,
            fill=1.0,
            base=0,
            pattern=[[-1, P]],
            channel_multiplier=1,
        )
        kw_table = on_table(0, [P, T], I32, "kw_table")
        nc.sync.dma_start(kw_table[:], k_words[0].rearrange("p n t -> p (n t)").bitcast(I32))
        v_tables = []
        for j in range(E_BLOCKS):
            v_table = on_table(1 + j, [P, T], F32, f"v_table{j}")
            nc.sync.dma_start(v_table[:], vT[j * P : (j + 1) * P, :])
            v_tables.append(v_table)

        us_step = own([P, PACK], F32, "us_step")
        nc.gpsimd.tensor_scalar(us_step[:], us_col[:], 0.0, 2.0, ALU.is_ge, ALU.mult)
        us_sign = own([P, PACK], BF16, "us_sign")
        nc.gpsimd.tensor_scalar(us_sign[:], us_step[:], 1.0, -1.0, ALU.mult, ALU.add)
        us_abs = own([P, PACK], F32, "us_abs")
        nc.gpsimd.tensor_tensor(us_abs[:], us_col[:], us_sign[:], ALU.mult)

        ks_listed = own([P, N], U8, "ks_listed")
        nc.vector.tensor_copy(ks_listed[:], ks_table[:].indirect(offsets[:]))
        nb_listed = own([P, N], F32, "nb_listed")
        nc.vector.tensor_copy(nb_listed[:], nb_table[:].indirect(offsets[:]))
        ks_dealt = on_nb(0, [P, N], U8, "ks_dealt")
        nc.vector.tensor_copy(
            ks_dealt[:].rearrange("p (t c i) -> p c t i", t=PACK, i=16),
            ks_listed[:].rearrange("p (c i t) -> p c t i", t=PACK, i=16),
        )

        q_woven = own([P, NQ, PACK], BF16, "q_woven")
        nc.scalar.copy(
            q_woven[:].rearrange("p (c i) t -> p c t i", i=4),
            q_raw[:].rearrange("p t (c i) -> p c t i", i=4),
        )
        q_mx = quantize(
            q_woven[:].rearrange("p q t -> p (q t)"),
            on_nb(N, [P, NQ], U32, "q_codes"),
            own([P, NQ], U8, "q_scales"),
        )
        kw_dealt = on_nb(N + NQ * 4, [P, N], U32, "kw_dealt")
        nc.vector.tensor_copy(
            kw_dealt[:].rearrange("p (t s) -> p s t", t=PACK),
            kw_table[:].bitcast(U32).indirect(offsets[:]),
        )

        nb_turned = bank(7, [P, PACK, P])
        for t in range(PACK):
            nc.tensor.transpose(nb_turned[:, t, :], nb_listed[:, t::PACK], ident[:])
        bias = own([P, PACK], F32, "bias")
        for t in range(PACK):
            nc.scalar.activation(
                bias[:, t : t + 1], nb_turned[:, t, NB_ROW : NB_ROW + 1], ACT.Copy, scale=us_abs[:, t : t + 1]
            )

        def first_layer(h):
            pairs = own([P, 2, QH, 2], BF16, f"y_pairs{h}")
            for t in range(PACK):
                a = bank(PACK * h + t, [P, QH])
                matmul(a[:], (kw_dealt, ks_dealt), slice(t * P, (t + 1) * P), q_mx, slice(h * QH, (h + 1) * QH))
                nc.scalar.activation(
                    pairs[:, t // 2, :, t % 2], a[:], ACT.Relu, bias=bias[:, t : t + 1], scale=us_abs[:, t : t + 1]
                )
            return pairs

        def weave_y(pairs, woven):
            nc.vector.tensor_tensor(
                woven[:],
                pairs[:].rearrange("p u q e -> p q u e"),
                us_sign[:].rearrange("p (u e) -> p u e", e=2).unsqueeze(1).to_broadcast([P, QH, 2, 2]),
                ALU.mult,
            )
            return woven[:].rearrange("p q u e -> p (q u e)")

        def gather_values(j, listed):
            nc.vector.tensor_copy(listed, v_tables[j][:].indirect(offsets[:]))
            return listed

        def turn_values(gathered, bank_index, name):
            turned = bank(bank_index, [P, len(gathered), 2, P])
            for j, listed in enumerate(gathered):
                for u in range(2):
                    nc.tensor.transpose(turned[:, j, u, :], listed.bitcast(F32)[:, u::2], ident[:])
            woven = own([P, len(gathered) * P * PACK], BF16, name)
            nc.scalar.copy(
                woven[:].bitcast(F32).rearrange("p (j e u) -> p j e u", e=P, u=2),
                turned[:].rearrange("p j u e -> p j e u"),
            )
            return woven[:]

        out_rows = out[0].rearrange("(b p) e -> p b e", p=P)
        y_mx = []

        def second_layer(v_mx, e0, q_blocks, bank_index, staged, copy, queue):
            width = v_mx[1].shape[1]
            acc = bank(bank_index, [P, len(q_blocks), width])
            for n, b in enumerate(q_blocks):
                h, c = divmod(b * P, QH)
                matmul(acc[:, n, :], y_mx[h], slice(c, c + P), v_mx, slice(0, width))
            copy(staged[:], acc[:])
            queue.dma_start(out_rows[:, q_blocks.start : q_blocks.stop, e0 : e0 + width], staged[:])

        pairs = [first_layer(h) for h in range(2)]
        listed01 = after("q_woven", [P, 2 * N], BF16, "v_listed01")
        v0 = gather_values(0, listed01[:, :N])
        v1 = gather_values(1, listed01[:, N:])
        y_woven0 = weave_y(pairs[0], on_table(2, [P, QH, 2, 2], BF16, "y_woven0"))
        y_mx.append(quantize(y_woven0, own([P, QH], U32, "y0_codes"), own([P, QH], U8, "y0_scales")))
        v_woven01 = turn_values([v0, v1], 5, "v_woven01")
        v2 = gather_values(2, after("y_pairs0", [P, N], BF16, "v_listed2")[:])
        v_woven2 = turn_values([v2], 6, "v_woven2")
        y_woven1 = weave_y(pairs[1], on_table(3, [P, QH, 2, 2], BF16, "y_woven1"))
        v01_mx = quantize(
            v_woven01, after("y_pairs1", [P, 2 * P], U32, "v01_codes"), own([P, 2 * P], U8, "v01_scales")
        )
        y_mx.append(quantize(y_woven1, own([P, QH], U32, "y1_codes"), own([P, QH], U8, "y1_scales")))
        v2_mx = quantize(v_woven2, after("v_woven01", [P, P], U32, "v2_codes"), own([P, P], U8, "v2_scales"))
        for half in range(2):
            staged = own([P, 2, 2 * P], F32, f"staged01_{half}")
            second_layer(v01_mx, 0, range(2 * half, 2 * half + 2), half, staged, nc.scalar.copy, nc.sync)
        v3 = gather_values(3, v_woven2)
        staged2 = on_table(4, [P, 4, P], F32, "staged2")
        second_layer(v2_mx, 2 * P, range(4), 2, staged2, nc.vector.tensor_copy, nc.sync)
        v_woven3 = turn_values([v3], 7, "v_woven3")
        v3_mx = quantize(v_woven3, own([P, P], U32, "v3_codes"), own([P, P], U8, "v3_scales"))
        second_layer(v3_mx, 3 * P, range(0, 2), 3, own([P, 2, P], F32, "staged3_0"), nc.vector.tensor_copy, nc.sync)
        second_layer(v3_mx, 3 * P, range(2, 4), 4, own([P, 2, P], F32, "staged3_1"), nc.scalar.copy, nc.scalar)
